import numpy as np
import ml_dtypes


def mxq(x, axis, fmt="e4m3"):
    dtype, down = {"e4m3": (ml_dtypes.float8_e4m3fn, 7), "e5m2": (ml_dtypes.float8_e5m2, 14)}[fmt]
    v = np.moveaxis(np.asarray(x, np.float32).astype(ml_dtypes.bfloat16).astype(np.float64), axis, -1)
    blocks = v.reshape(v.shape[:-1] + (-1, 32))
    amax = np.abs(blocks).max(-1, keepdims=True)
    byte = np.maximum(np.where(amax > 0, np.frexp(amax)[1] - 1 + 127, 0) - down, 1)
    scale = np.exp2(byte - 127.0)
    codes = (blocks / scale).astype(np.float32).astype(dtype).astype(np.float64)
    return np.moveaxis((codes * scale).reshape(v.shape), -1, axis)


WIDE = False


def mx_kscale(k):
    if not WIDE:
        return np.ones(k)
    levels = np.array([10, -10, 5, -5, 0])
    if k % 512:
        return np.exp2(np.random.permutation(np.resize(levels, k // 32))).repeat(32)
    a = np.empty((k // 512, 16))
    for p in range(k // 512):
        a[p, :8] = np.random.permutation(np.resize(levels, 8))
        for g in range(8):
            far = levels[np.abs(levels - a[p, g]) >= 10]
            a[p, g + 8] = far[np.random.randint(len(far))]
    return np.exp2(a.ravel()).repeat(32)


def f64(x):
    return np.asarray(x).astype(np.float64)


def striped(idx):
    return np.tile(idx.reshape(-1, 16).T, (8, 1)).astype(np.uint16)


def unstriped(offs):
    return offs[:16].T.reshape(-1).astype(np.int64)


def striped8(idx):
    return np.concatenate([x.reshape(-1, 16).T for x in idx]).astype(np.uint16)


def runs(offs, k):
    lists = np.stack([offs[16 * r : 16 * r + 16].T.reshape(-1) for r in range(8)]).astype(np.int64)
    return lists[np.arange(k) % 512 // 64]


def pack_weight(w):
    k, n = w.shape
    w = f64(np.asarray(w, np.float32).astype(ml_dtypes.bfloat16)).reshape(k // 32, 32, n)
    amax = np.abs(w).max(1)
    byte = np.clip(np.where(amax > 0, np.frexp(amax)[1] - 1 + 127 - 7, 1), 1, 254)
    scaled = (w * np.exp2(127.0 - byte)[:, None, :]).reshape(k, n).astype(np.float32)
    words = np.ascontiguousarray(scaled.reshape(k // 512, 128, 4, n).transpose(0, 1, 3, 2)).astype(ml_dtypes.float8_e4m3fn).view(np.uint8)
    return words, np.ascontiguousarray(byte.astype(np.uint8).reshape(k // 512, 16, n))


def unpack_weight(words, scales):
    g, p, n, _ = words.shape
    vals = np.ascontiguousarray(words).view(ml_dtypes.float8_e4m3fn).astype(np.float64) * np.repeat(np.exp2(scales.astype(np.float64) - 127.0), 8, axis=1)[..., None]
    return vals.transpose(0, 1, 3, 2).reshape(g * 512, n)


def sigmoid(v):
    return 1.0 / (1.0 + np.exp(-np.maximum(v, -700.0)))


K, T, S, N, H, W = 512, 2048, 512, 512, 512, 256


def setup_inputs():
    n = np.random.standard_normal
    s = mx_kscale(K)[:, None]
    u = mx_kscale(H)
    packed_xT = pack_weight(n((K, T)) * s)
    perm = np.stack([np.random.permutation(S) for _ in range(8)])
    perm2 = np.stack([np.random.permutation(S) for _ in range(8)])
    return {
        "x_words": packed_xT[0],
        "x_scales": packed_xT[1],
        "w1": (n((K, H)) / np.sqrt(K) / s).astype(np.float32),
        "gn": (np.random.uniform(0.5, 1.5, (H, 1)) * u[:, None]).astype(np.float32),
        "gm": (np.random.uniform(0.5, 1.5, (H, 1)) * u[:, None]).astype(np.float32),
        "w2": (n((H, N)) / np.sqrt(2 * H) / u[:, None]).astype(np.float32),
        "w3": (n((H, N)) / np.sqrt(2 * H) / u[:, None]).astype(np.float32),
        "offs": striped(np.random.permutation(T)[:S]),
        "n1": striped8(np.stack([np.random.permutation(S) for _ in range(8)])),
        "n2": striped8(np.stack([np.random.permutation(S) for _ in range(8)])),
        "n3": striped8(perm[:, :W]),
        "n4": striped8(perm[:, W:]),
        "n5": striped8(perm2[:, :W]),
        "n6": striped8(perm2[:, W:]),
    }


def reference(x_words, x_scales, w1, gn, gm, w2, w3, offs, n1, n2, n3, n4, n5, n6):
    xq = unpack_weight(x_words, x_scales)[:, unstriped(offs)]
    y = mxq(f64(w1), 0, "e4m3").T @ xq
    ex = np.exp(0.5 * y)
    z = f64(gn) * ((2.0 * ex) / (ex + ex[np.arange(H)[:, None], runs(n1, H)] + ex[np.arange(H)[:, None], runs(n2, H)]))
    pb = y[np.arange(H)[:, None], runs(n4, H)]
    pa = y[np.arange(H)[:, None], runs(n3, H)]
    rb = pb * sigmoid(pb - pa)
    ra = pa * sigmoid(pa - pb)
    ds = np.zeros((H, S))
    ds[np.arange(H)[:, None], runs(n3, H)] = ra
    dt = ds.copy()
    dt[np.arange(H)[:, None], runs(n4, H)] = rb
    z2 = f64(gm) * dt
    h = mxq(f64(w2), 0, "e4m3").T @ mxq(z, 0, "e4m3") + mxq(f64(w3), 0, "e4m3").T @ mxq(z2, 0, "e4m3")
    pa2 = h[np.arange(N)[:, None], runs(n5, N)]
    pb2 = h[np.arange(N)[:, None], runs(n6, N)]
    rb2 = np.minimum(pa2, pb2)
    ra2 = np.maximum(pa2, pb2)
    ds2 = np.zeros((N, S))
    ds2[np.arange(N)[:, None], runs(n5, N)] = ra2
    out = ds2.copy()
    out[np.arange(N)[:, None], runs(n6, N)] = rb2
    return out

@@ -1,0 +1,251 @@
+from contextlib import ExitStack
+
+import concourse.mybir as mybir
+from concourse.masks import make_identity
+
+K, T, S, H, N, W = 512, 2048, 512, 512, 512, 256
+FLOPS = 2 * K * H * S + 2 * 2 * H * N * S
+
+F32 = mybir.dt.float32
+BF16 = mybir.dt.bfloat16
+I32 = mybir.dt.int32
+U32 = mybir.dt.uint32
+U16 = mybir.dt.uint16
+U8 = mybir.dt.uint8
+FP8X4 = mybir.dt.float8_e4m3fn_x4
+ALU = mybir.AluOpType
+ACT = mybir.ActivationFunctionType
+
+P = 128
+PACK = 4
+W1_VECTOR_M = 88
+HALVES = (slice(0, S // 2), slice(S // 2, S))
+WHOLE = (slice(0, S),)
+
+
+def tile_picked_joinshareduelorder_none_p_kernel(
+    tc, x_words, x_scales, w1, gn, gm, w2, w3, offs, n1, n2, n3, n4, n5, n6, out
+):
+    nc = tc.nc
+    tiles = range(PACK)
+
+    with ExitStack() as ctx:
+        keep = ctx.enter_context(tc.tile_pool(name="keep", bufs=1))
+        psum = ctx.enter_context(tc.psum_pool(name="psum", bufs=PACK))
+
+        def per_tile(name, width, dtype=F32):
+            return [keep.tile([P, width], dtype, name=f"{name}{t}", tag=f"{name}{t}", align_bytes=64) for t in tiles]
+
+        def load_list(name, src):
+            tile = keep.tile(list(src.shape), U16, name=name)
+            nc.sync.dma_start(tile[:], src)
+            return tile
+
+        def load_weight(name, src):
+            raw = keep.tile([P, PACK, src.shape[1]], F32, name=name, align_bytes=64)
+            nc.sync.dma_start(raw[:], src.rearrange("(p j) c -> p j c", j=PACK))
+            return raw
+
+        def load_gain(name, src):
+            gain = keep.tile([P, PACK], F32, name=name)
+            nc.sync.dma_start(gain[:], src.rearrange("(p t) o -> p (t o)", t=PACK))
+            return gain
+
+        def entries(lst, cols):
+            return lst[:, cols.start // 16 : cols.stop // 16]
+
+        def mx_tiles(name, width):
+            codes = keep.tile([P, width], U32, name=f"{name}_codes", align_bytes=64)
+            scales = keep.tile([P, width], U8, name=f"{name}_scales", align_bytes=64)
+            return codes, scales
+
+        def quantize(mx, src, cols):
+            nc.vector.quantize_mx(
+                out=mx[0][:, cols].bitcast(FP8X4),
+                scales=mx[1][:, cols],
+                in_=src[:, PACK * cols.start : PACK * cols.stop],
+            )
+
+        def product(acc, weights, t, moving, cols, start, stop):
+            rows = slice(P * t, P * (t + 1))
+            nc.tensor.matmul_mx(
+                out=acc[:, cols],
+                lhsT=weights[0][:, rows].bitcast(FP8X4),
+                lhsT_scale=weights[1][:, rows],
+                rhs=moving[0][:, cols].bitcast(FP8X4),
+                rhs_scale=moving[1][:, cols],
+                start=start,
+                stop=stop,
+            )
+
+        def weave(dst, planes, cols):
+            nc.vector.tensor_copy(
+                out=dst[:, PACK * cols.start : PACK * cols.stop].rearrange("p (c i t) -> p c t i", i=PACK, t=PACK),
+                in_=planes[:, :, cols].rearrange("p t (c i) -> p c t i", i=PACK),
+            )
+
+        def turn(acc, terms):
+            for b in range(acc.shape[1] // P):
+                cols = slice(P * b, P * (b + 1))
+                for i, term in enumerate(terms):
+                    nc.tensor.matmul(
+                        acc[:, cols], term[:, cols], ident[:], start=i == 0, stop=i == len(terms) - 1, is_transpose=True
+                    )
+
+        table_scales = keep.tile([P, T], U8, align_bytes=64)
+        nc.vector.memset(table_scales[:].bitcast(I32), 0)
+        w1_raw = load_weight("w1_raw", w1)
+        for q in range(4):
+            nc.sync.dma_start(
+                table_scales[32 * q : 32 * q + 4, :].bitcast(I32), x_scales[0, 4 * q : 4 * q + 4, :].bitcast(I32)
+            )
+        offs_sb = load_list("offs_sb", offs)
+        table_words = keep.tile([P, T], U32, align_bytes=64)
+        nc.sync.dma_start(table_words[:].bitcast(I32), x_words[0].rearrange("p n t -> p (n t)").bitcast(I32))
+        n3_sb = load_list("n3_sb", n3)
+        n4_sb = load_list("n4_sb", n4)
+        gm_sb = load_gain("gm_sb", gm)
+        n1_sb = load_list("n1_sb", n1)
+        n2_sb = load_list("n2_sb", n2)
+        w2_raw = load_weight("w2_raw", w2)
+        gn_sb = load_gain("gn_sb", gn)
+        w3_raw = load_weight("w3_raw", w3)
+        n5_sb = load_list("n5_sb", n5)
+        n6_sb = load_list("n6_sb", n6)
+
+        ident = keep.tile([P, P], F32, align_bytes=64)
+        make_identity(nc, ident[:])
+        half_gm = keep.tile([P, PACK], F32)
+        minus_half_gm = keep.tile([P, PACK], F32)
+        twice_gn = keep.tile([P, PACK], F32)
+        nc.gpsimd.tensor_scalar(half_gm[:], gm_sb[:], 0.5, 0.0, ALU.mult, ALU.add)
+        nc.gpsimd.tensor_scalar(minus_half_gm[:], gm_sb[:], -0.5, 0.0, ALU.mult, ALU.add)
+        nc.gpsimd.tensor_scalar(twice_gn[:], gn_sb[:], 2.0, 0.0, ALU.mult, ALU.add)
+
+        w1_dealt = keep.tile([P, PACK * H], BF16, align_bytes=64)
+        dst = w1_dealt[:].rearrange("p (t m j) -> p m t j", t=PACK, j=PACK)
+        src = w1_raw[:].rearrange("p j (m t) -> p m t j", t=PACK)
+        nc.vector.tensor_copy(out=dst[:, :W1_VECTOR_M], in_=src[:, :W1_VECTOR_M])
+        nc.scalar.copy(out=dst[:, W1_VECTOR_M:], in_=src[:, W1_VECTOR_M:])
+        w1_mx = mx_tiles("w1", H)
+        picked = mx_tiles("picked", S)
+        nc.vector.tensor_copy(picked[1][:], table_scales[:].indirect(offs_sb[:]))
+        quantize(w1_mx, w1_dealt, slice(0, H))
+        for cols in HALVES:
+            nc.vector.tensor_copy(picked[0][:, cols], table_words[:].indirect(entries(offs_sb, cols)))
+
+        y = per_tile("y", S)
+        for t in tiles:
+            y_acc = psum.tile([P, S], F32, tag="rows")
+            for cols in HALVES if t == 0 else WHOLE:
+                product(y_acc, w1_mx, t, picked, cols, True, True)
+                nc.scalar.copy(out=y[t][:, cols], in_=y_acc[:, cols])
+
+        pa, minus_pb, th_turned = (per_tile(name, W) for name in ("pa", "minus_pb", "th_turned"))
+        share_a, minus_share_b = per_tile("share_a", W), per_tile("minus_share_b", W)
+        for t in tiles:
+            nc.vector.tensor_copy(pa[t][:], y[t][:].indirect(n3_sb[:]))
+            nc.vector.tensor_scalar(minus_pb[t][:], y[t][:].indirect(n4_sb[:]), -1.0, 0.0, ALU.mult, ALU.add)
+            duel_acc = psum.tile([P, 2 * W], F32, tag="rows")
+            turn(duel_acc[:, :W], (pa[t], minus_pb[t]))
+            nc.scalar.activation(th_turned[t][:], duel_acc[:, :W], ACT.Tanh, scale=0.5)
+            turn(duel_acc[:, W:], (th_turned[t],))
+            col = slice(t, t + 1)
+            nc.scalar.activation(
+                share_a[t][:], duel_acc[:, W:], ACT.Identity, bias=half_gm[:, col], scale=half_gm[:, col]
+            )
+            nc.scalar.activation(
+                minus_share_b[t][:], duel_acc[:, W:], ACT.Identity, bias=minus_half_gm[:, col], scale=half_gm[:, col]
+            )
+
+        w2_dealt = keep.tile([P, PACK * N], BF16, align_bytes=64)
+        w3_dealt = keep.tile([P, PACK * N], BF16, align_bytes=64)
+
+        def deal_views(dealt, raw):
+            return (
+                dealt[:].rearrange("p (t m j) -> p m t j", t=PACK, j=PACK),
+                raw[:].rearrange("p j (m t) -> p m t j", t=PACK),
+            )
+
+        e1, e2 = per_tile("e1", S), per_tile("e2", S)
+        sums = []
+        for t in tiles:
+            for e, lst in ((e1, n1_sb), (e2, n2_sb)):
+                for cols in HALVES:
+                    nc.scalar.activation(e[t][:, cols], y[t][:].indirect(entries(lst, cols)), ACT.Exp, scale=0.5)
+            sum_acc = psum.tile([P, S], F32, tag="turned")
+            turn(sum_acc[:], (e1[t], e2[t]))
+            sums.append(sum_acc)
+
+        z2 = per_tile("z2", S)
+        for step in range(PACK + 1):
+            if step < PACK:
+                nc.vector.tensor_tensor(z2[step][:].indirect(n3_sb[:]), pa[step][:], share_a[step][:], ALU.mult)
+            if step > 0:
+                t = step - 1
+                nc.vector.tensor_tensor(z2[t][:].indirect(n4_sb[:]), minus_pb[t][:], minus_share_b[t][:], ALU.mult)
+
+        log_turned, logit, share = per_tile("log_turned", S), per_tile("logit", S), per_tile("share", S)
+        for t in tiles:
+            nc.scalar.activation(log_turned[t][:], sums[t][:], ACT.Ln)
+        for t in tiles:
+            log_acc = psum.tile([P, S], F32, tag="rows")
+            turn(log_acc[:], (log_turned[t],))
+            nc.vector.scalar_tensor_tensor(logit[t][:], y[t][:], 0.5, log_acc[:], ALU.mult, ALU.subtract)
+
+        dst, src = deal_views(w3_dealt, w3_raw)
+        nc.scalar.copy(out=dst, in_=src)
+        dst, src = deal_views(w2_dealt, w2_raw)
+        nc.vector.tensor_copy(out=dst, in_=src)
+
+        w2_mx, w3_mx = mx_tiles("w2", N), mx_tiles("w3", N)
+        quantize(w2_mx, w2_dealt, slice(0, N))
+
+        z2_planes = keep.tile([P, PACK, S], BF16, tag="y0", align_bytes=64)
+        for t in tiles:
+            nc.vector.tensor_copy(out=z2_planes[:, t, :], in_=z2[t][:])
+        z2_woven = keep.tile([P, PACK * S], BF16, align_bytes=64)
+        weave(z2_woven, z2_planes, slice(0, S))
+        quantize(w3_mx, w3_dealt, slice(0, N))
+        z2_mx = mx_tiles("z2", S)
+        quantize(z2_mx, z2_woven, slice(0, S))
+
+        z_planes = keep.tile([P, PACK, S], BF16, align_bytes=64)
+        for t in tiles:
+            nc.scalar.activation(share[t][:], logit[t][:], ACT.Sigmoid)
+        for t in tiles:
+            if t < 2:
+                nc.scalar.activation(z_planes[:, t, :], share[t][:], ACT.Copy, scale=twice_gn[:, t : t + 1])
+            else:
+                nc.vector.tensor_scalar(z_planes[:, t, :], share[t][:], twice_gn[:, t : t + 1], None, ALU.mult)
+        z_woven = keep.tile([P, PACK * S], BF16, align_bytes=64)
+        z_mx = mx_tiles("z", S)
+        for cols in HALVES:
+            weave(z_woven, z_planes, cols)
+        for cols in HALVES:
+            quantize(z_mx, z_woven, cols)
+
+        h, result = per_tile("h", S), per_tile("result", S)
+        for t in tiles:
+            h_acc = psum.tile([P, S], F32, tag="turned")
+            for cols in HALVES if t == 0 else WHOLE:
+                product(h_acc, w3_mx, t, z2_mx, cols, True, False)
+                product(h_acc, w2_mx, t, z_mx, cols, False, True)
+                nc.scalar.copy(out=h[t][:, cols], in_=h_acc[:, cols])
+
+        out_rows = out.rearrange("(p t) n -> t p n", t=PACK)
+
+        pa2, lead, rise, drop, fall = (per_tile(name, W) for name in ("pa2", "lead", "rise", "drop", "fall"))
+        for t in tiles:
+            nc.vector.tensor_copy(pa2[t][:], h[t][:].indirect(n5_sb[:]))
+            nc.vector.tensor_tensor(lead[t][:], h[t][:].indirect(n6_sb[:]), pa2[t][:], ALU.subtract)
+            nc.scalar.activation(rise[t][:], lead[t][:], ACT.Relu)
+            nc.scalar.activation(drop[t][:], lead[t][:], ACT.Relu, scale=-1.0)
+            nc.scalar.mul(fall[t][:], drop[t][:], -1.0)
+        for step in range(PACK + 1):
+            if step < PACK:
+                nc.vector.tensor_tensor(result[step][:].indirect(n5_sb[:]), pa2[step][:], rise[step][:], ALU.add)
+            if step > 0:
+                t = step - 1
+                nc.vector.tensor_tensor(result[t][:].indirect(n6_sb[:]), pa2[t][:], fall[t][:], ALU.add)
+                nc.sync.dma_start(out_rows[t], result[t][:])

@@ -18,8 +18,8 @@ ACT = mybir.ActivationFunctionType
 
 P = 128
 PACK = 4
-W1_VECTOR_M = 88
 HALVES = (slice(0, S // 2), slice(S // 2, S))
+PIECES = HALVES
 WHOLE = (slice(0, S),)
 
 
@@ -41,8 +41,8 @@ def tile_picked_joinshareduelorder_none_p_kernel(
             nc.sync.dma_start(tile[:], src)
             return tile
 
-        def load_weight(name, src):
-            raw = keep.tile([P, PACK, src.shape[1]], F32, name=name, align_bytes=64)
+        def load_weight(name, src, tag):
+            raw = keep.tile([P, PACK, src.shape[1]], F32, name=name, tag=tag, align_bytes=64)
             nc.sync.dma_start(raw[:], src.rearrange("(p j) c -> p j c", j=PACK))
             return raw
 
@@ -94,22 +94,22 @@ def tile_picked_joinshareduelorder_none_p_kernel(
 
         table_scales = keep.tile([P, T], U8, align_bytes=64)
         nc.vector.memset(table_scales[:].bitcast(I32), 0)
-        w1_raw = load_weight("w1_raw", w1)
+        offs_sb = load_list("offs_sb", offs)
+        w1_raw = load_weight("w1_raw", w1, "w1_raw")
         for q in range(4):
             nc.sync.dma_start(
                 table_scales[32 * q : 32 * q + 4, :].bitcast(I32), x_scales[0, 4 * q : 4 * q + 4, :].bitcast(I32)
             )
-        offs_sb = load_list("offs_sb", offs)
-        table_words = keep.tile([P, T], U32, align_bytes=64)
-        nc.sync.dma_start(table_words[:].bitcast(I32), x_words[0].rearrange("p n t -> p (n t)").bitcast(I32))
         n3_sb = load_list("n3_sb", n3)
         n4_sb = load_list("n4_sb", n4)
-        gm_sb = load_gain("gm_sb", gm)
+        table_words = keep.tile([P, T], U32, align_bytes=64)
+        nc.sync.dma_start(table_words[:].bitcast(I32), x_words[0].rearrange("p n t -> p (n t)").bitcast(I32))
         n1_sb = load_list("n1_sb", n1)
+        gm_sb = load_gain("gm_sb", gm)
         n2_sb = load_list("n2_sb", n2)
-        w2_raw = load_weight("w2_raw", w2)
+        w2_raw = load_weight("w2_raw", w2, "w2_raw")
         gn_sb = load_gain("gn_sb", gn)
-        w3_raw = load_weight("w3_raw", w3)
+        w3_raw = load_weight("w3_raw", w3, "w3_raw")
         n5_sb = load_list("n5_sb", n5)
         n6_sb = load_list("n6_sb", n6)
 
@@ -122,59 +122,76 @@ def tile_picked_joinshareduelorder_none_p_kernel(
         nc.gpsimd.tensor_scalar(minus_half_gm[:], gm_sb[:], -0.5, 0.0, ALU.mult, ALU.add)
         nc.gpsimd.tensor_scalar(twice_gn[:], gn_sb[:], 2.0, 0.0, ALU.mult, ALU.add)
 
-        w1_dealt = keep.tile([P, PACK * H], BF16, align_bytes=64)
-        dst = w1_dealt[:].rearrange("p (t m j) -> p m t j", t=PACK, j=PACK)
-        src = w1_raw[:].rearrange("p j (m t) -> p m t j", t=PACK)
-        nc.vector.tensor_copy(out=dst[:, :W1_VECTOR_M], in_=src[:, :W1_VECTOR_M])
-        nc.scalar.copy(out=dst[:, W1_VECTOR_M:], in_=src[:, W1_VECTOR_M:])
-        w1_mx = mx_tiles("w1", H)
         picked = mx_tiles("picked", S)
         nc.vector.tensor_copy(picked[1][:], table_scales[:].indirect(offs_sb[:]))
-        quantize(w1_mx, w1_dealt, slice(0, H))
+        w1_mx = mx_tiles("w1", H)
+        for t0, t1, copy in ((0, 2, nc.vector.tensor_copy), (2, PACK, nc.scalar.copy)):
+            w1_dealt = keep.tile([P, (t1 - t0) * PACK * P], BF16, name=f"w1_dealt{t0}", align_bytes=64)
+            copy(
+                out=w1_dealt[:].rearrange("p (t m j) -> p m t j", m=P, j=PACK),
+                in_=w1_raw[:].rearrange("p j (m t) -> p m t j", t=PACK)[:, :, t0:t1],
+            )
+            nc.vector.quantize_mx(
+                out=w1_mx[0][:, P * t0 : P * t1].bitcast(FP8X4), scales=w1_mx[1][:, P * t0 : P * t1], in_=w1_dealt[:]
+            )
         for cols in HALVES:
             nc.vector.tensor_copy(picked[0][:, cols], table_words[:].indirect(entries(offs_sb, cols)))
 
-        y = per_tile("y", S)
+        y = per_tile("y", 2 * S)
         for t in tiles:
-            y_acc = psum.tile([P, S], F32, tag="rows")
+            nc.gpsimd.memset(y[t][:, S:], 0.0)
+        for t in tiles:
             for cols in HALVES if t == 0 else WHOLE:
+                y_acc = psum.tile([P, S], F32, tag="turned", bufs=5)
                 product(y_acc, w1_mx, t, picked, cols, True, True)
-                nc.scalar.copy(out=y[t][:, cols], in_=y_acc[:, cols])
+                copy = nc.vector.tensor_copy if t >= 3 else nc.scalar.copy
+                copy(out=y[t][:, cols], in_=y_acc[:, cols])
 
         pa, minus_pb, th_turned = (per_tile(name, W) for name in ("pa", "minus_pb", "th_turned"))
-        share_a, minus_share_b = per_tile("share_a", W), per_tile("minus_share_b", W)
+        share_a, minus_share_b = per_tile("share_a", W), []
         for t in tiles:
             nc.vector.tensor_copy(pa[t][:], y[t][:].indirect(n3_sb[:]))
             nc.vector.tensor_scalar(minus_pb[t][:], y[t][:].indirect(n4_sb[:]), -1.0, 0.0, ALU.mult, ALU.add)
-            duel_acc = psum.tile([P, 2 * W], F32, tag="rows")
-            turn(duel_acc[:, :W], (pa[t], minus_pb[t]))
-            nc.scalar.activation(th_turned[t][:], duel_acc[:, :W], ACT.Tanh, scale=0.5)
-            turn(duel_acc[:, W:], (th_turned[t],))
+
+        ex, e1, e2 = per_tile("ex", S), per_tile("e1", S), per_tile("e2", S)
+
+        def exp_at(e, lst, t, cols):
+            nc.scalar.activation(e[t][:, cols], y[t][:].indirect(entries(lst, cols)), ACT.Exp, scale=0.5)
+
+        def share_b(t):
+            minus_share_b.append(keep.tile([P, W], F32, name=f"minus_share_b{t}", tag=f"th_turned{t + 1}", align_bytes=64))
+            nc.scalar.activation(
+                minus_share_b[t][:],
+                duel_acc[t][:],
+                ACT.Identity,
+                bias=minus_half_gm[:, t : t + 1],
+                scale=half_gm[:, t : t + 1],
+            )
+
+        look_ups = [(e, lst, t, WHOLE[0]) for t in tiles for e, lst in ((e1, n1_sb), (e2, n2_sb))]
+        duel_acc = []
+        for t in tiles:
             col = slice(t, t + 1)
+            lead_acc = psum.tile([P, W], F32, tag="lead", bufs=1)
+            duel_acc.append(psum.tile([P, W], F32, tag="rows", bufs=2, name=f"duel_acc{t}"))
+            turn(lead_acc[:], (pa[t], minus_pb[t]))
+            nc.scalar.activation(th_turned[t][:], lead_acc[:], ACT.Tanh, scale=0.5)
+            turn(duel_acc[t][:], (th_turned[t],))
+            exp_at(*look_ups[t])
             nc.scalar.activation(
-                share_a[t][:], duel_acc[:, W:], ACT.Identity, bias=half_gm[:, col], scale=half_gm[:, col]
+                share_a[t][:], duel_acc[t][:], ACT.Identity, bias=half_gm[:, col], scale=half_gm[:, col]
             )
-            nc.scalar.activation(
-                minus_share_b[t][:], duel_acc[:, W:], ACT.Identity, bias=minus_half_gm[:, col], scale=half_gm[:, col]
-            )
+            if t > 0:
+                share_b(t - 1)
+            nc.scalar.activation(ex[t][:], y[t][:, :S], ACT.Exp, scale=0.5)
+        share_b(PACK - 1)
 
-        w2_dealt = keep.tile([P, PACK * N], BF16, align_bytes=64)
-        w3_dealt = keep.tile([P, PACK * N], BF16, align_bytes=64)
-
-        def deal_views(dealt, raw):
-            return (
-                dealt[:].rearrange("p (t m j) -> p m t j", t=PACK, j=PACK),
-                raw[:].rearrange("p j (m t) -> p m t j", t=PACK),
-            )
-
-        e1, e2 = per_tile("e1", S), per_tile("e2", S)
         sums = []
         for t in tiles:
-            for e, lst in ((e1, n1_sb), (e2, n2_sb)):
-                for cols in HALVES:
-                    nc.scalar.activation(e[t][:, cols], y[t][:].indirect(entries(lst, cols)), ACT.Exp, scale=0.5)
-            sum_acc = psum.tile([P, S], F32, tag="turned")
-            turn(sum_acc[:], (e1[t], e2[t]))
+            for look_up in look_ups[max(2 * t, PACK) : 2 * t + 2]:
+                exp_at(*look_up)
+            sum_acc = psum.tile([P, S], F32, tag="turned", bufs=5)
+            turn(sum_acc[:], (ex[t], e1[t], e2[t]))
             sums.append(sum_acc)
 
         z2 = per_tile("z2", S)
@@ -185,52 +202,67 @@ def tile_picked_joinshareduelorder_none_p_kernel(
                 t = step - 1
                 nc.vector.tensor_tensor(z2[t][:].indirect(n4_sb[:]), minus_pb[t][:], minus_share_b[t][:], ALU.mult)
 
-        log_turned, logit, share = per_tile("log_turned", S), per_tile("logit", S), per_tile("share", S)
+        root_turned, inverse_turned = per_tile("root_turned", S), per_tile("inverse_turned", S)
+        z_planes = keep.tile([P, PACK, S], BF16, tag="z_planes", align_bytes=64)
         for t in tiles:
-            nc.scalar.activation(log_turned[t][:], sums[t][:], ACT.Ln)
-        for t in tiles:
-            log_acc = psum.tile([P, S], F32, tag="rows")
-            turn(log_acc[:], (log_turned[t],))
-            nc.vector.scalar_tensor_tensor(logit[t][:], y[t][:], 0.5, log_acc[:], ALU.mult, ALU.subtract)
-
-        dst, src = deal_views(w3_dealt, w3_raw)
-        nc.scalar.copy(out=dst, in_=src)
-        dst, src = deal_views(w2_dealt, w2_raw)
-        nc.vector.tensor_copy(out=dst, in_=src)
-
-        w2_mx, w3_mx = mx_tiles("w2", N), mx_tiles("w3", N)
-        quantize(w2_mx, w2_dealt, slice(0, N))
-
-        z2_planes = keep.tile([P, PACK, S], BF16, tag="y0", align_bytes=64)
-        for t in tiles:
-            nc.vector.tensor_copy(out=z2_planes[:, t, :], in_=z2[t][:])
-        z2_woven = keep.tile([P, PACK * S], BF16, align_bytes=64)
-        weave(z2_woven, z2_planes, slice(0, S))
-        quantize(w3_mx, w3_dealt, slice(0, N))
-        z2_mx = mx_tiles("z2", S)
-        quantize(z2_mx, z2_woven, slice(0, S))
-
-        z_planes = keep.tile([P, PACK, S], BF16, align_bytes=64)
-        for t in tiles:
-            nc.scalar.activation(share[t][:], logit[t][:], ACT.Sigmoid)
-        for t in tiles:
-            if t < 2:
-                nc.scalar.activation(z_planes[:, t, :], share[t][:], ACT.Copy, scale=twice_gn[:, t : t + 1])
+            nc.scalar.activation(root_turned[t][:], sums[t][:], ACT.Abs_reciprocal_sqrt)
+            back_acc = psum.tile([P, S], F32, tag="turned", bufs=5)
+            gain = twice_gn[:, t : t + 1]
+            if t in ():
+                turn(back_acc[:], (root_turned[t],))
+                nc.vector.scalar_tensor_tensor(inverse_turned[t][:], back_acc[:], gain, ex[t][:], ALU.mult, ALU.mult)
+                nc.vector.tensor_tensor(z_planes[:, t, :], inverse_turned[t][:], back_acc[:], ALU.mult)
             else:
-                nc.vector.tensor_scalar(z_planes[:, t, :], share[t][:], twice_gn[:, t : t + 1], None, ALU.mult)
+                nc.scalar.activation(inverse_turned[t][:], root_turned[t][:], ACT.Square)
+                turn(back_acc[:], (inverse_turned[t],))
+                nc.vector.scalar_tensor_tensor(z_planes[:, t, :], back_acc[:], gain, ex[t][:], ALU.mult, ALU.mult)
+
+        z2_planes = keep.tile([P, PACK, S], BF16, tag="share_a3", align_bytes=64)
+        for t in tiles:
+            if t < PACK - 0:
+                nc.vector.tensor_copy(out=z2_planes[:, t, :], in_=z2[t][:])
+            else:
+                nc.scalar.copy(out=z2_planes[:, t, :], in_=z2[t][:])
+        dealt = []
+        for t0 in (0, 2):
+            pair = keep.tile([P, 2, 2, PACK * P], BF16, name=f"dealt{t0}", tag=f"root_turned{t0 // 2 + 2}", align_bytes=64)
+            for which, raw in enumerate((w2_raw, w3_raw)):
+                nc.scalar.copy(
+                    out=pair[:, :, which, :].rearrange("p t (m j) -> p m t j", j=PACK),
+                    in_=raw[:].rearrange("p j (m t) -> p m t j", t=PACK)[:, :, t0 : t0 + 2],
+                )
+            dealt.extend(pair[:, i].rearrange("p w c -> p (w c)") for i in range(2))
+        z2_woven = keep.tile([P, PACK * S], BF16, align_bytes=64)
+        z2_mx = mx_tiles("z2", S)
         z_woven = keep.tile([P, PACK * S], BF16, align_bytes=64)
         z_mx = mx_tiles("z", S)
-        for cols in HALVES:
+        first_mx = mx_tiles("w23_first", 2 * P)
+        weave(z2_woven, z2_planes, slice(0, S))
+        quantize(first_mx, dealt[0], slice(0, 2 * P))
+        quantize(z2_mx, z2_woven, slice(0, S))
+        for cols in PIECES:
             weave(z_woven, z_planes, cols)
-        for cols in HALVES:
+        for cols in PIECES:
             quantize(z_mx, z_woven, cols)
+        rest_mx = (
+            keep.tile([P, 6 * P], U32, name="w23_rest_codes", tag="z_planes", align_bytes=64),
+            keep.tile([P, 6 * P], U8, name="w23_rest_scales", align_bytes=64),
+        )
+        for t in range(1, PACK):
+            cols = slice(2 * P * (t - 1), 2 * P * t)
+            nc.vector.quantize_mx(
+                out=rest_mx[0][:, cols].bitcast(FP8X4),
+                scales=rest_mx[1][:, cols],
+                in_=dealt[t],
+            )
 
         h, result = per_tile("h", S), per_tile("result", S)
         for t in tiles:
-            h_acc = psum.tile([P, S], F32, tag="turned")
-            for cols in HALVES if t == 0 else WHOLE:
-                product(h_acc, w3_mx, t, z2_mx, cols, True, False)
-                product(h_acc, w2_mx, t, z_mx, cols, False, True)
+            weights, block = (first_mx, 0) if t == 0 else (rest_mx, 2 * (t - 1))
+            for cols in PIECES if t == 0 else WHOLE:
+                h_acc = psum.tile([P, S], F32, tag="turned", bufs=5)
+                product(h_acc, weights, block, z_mx, cols, True, False)
+                product(h_acc, weights, block + 1, z2_mx, cols, False, True)
                 nc.scalar.copy(out=h[t][:, cols], in_=h_acc[:, cols])
 
         out_rows = out.rearrange("(p t) n -> t p n", t=PACK)

@@ -18,6 +18,7 @@ ACT = mybir.ActivationFunctionType
 
 P = 128
 PACK = 4
+W1_VECTOR_M = 64
 HALVES = (slice(0, S // 2), slice(S // 2, S))
 PIECES = HALVES
 WHOLE = (slice(0, S),)
@@ -92,6 +93,12 @@ def tile_picked_joinshareduelorder_none_p_kernel(
                         acc[:, cols], term[:, cols], ident[:], start=i == 0, stop=i == len(terms) - 1, is_transpose=True
                     )
 
+        def deal_views(dealt, raw):
+            return (
+                dealt[:].rearrange("p (t m j) -> p m t j", t=PACK, j=PACK),
+                raw[:].rearrange("p j (m t) -> p m t j", t=PACK),
+            )
+
         table_scales = keep.tile([P, T], U8, align_bytes=64)
         nc.vector.memset(table_scales[:].bitcast(I32), 0)
         offs_sb = load_list("offs_sb", offs)
@@ -107,8 +114,8 @@ def tile_picked_joinshareduelorder_none_p_kernel(
         n1_sb = load_list("n1_sb", n1)
         gm_sb = load_gain("gm_sb", gm)
         n2_sb = load_list("n2_sb", n2)
-        w2_raw = load_weight("w2_raw", w2, "w2_raw")
         gn_sb = load_gain("gn_sb", gn)
+        w2_raw = load_weight("w2_raw", w2, "w2_raw")
         w3_raw = load_weight("w3_raw", w3, "w3_raw")
         n5_sb = load_list("n5_sb", n5)
         n6_sb = load_list("n6_sb", n6)
@@ -118,22 +125,18 @@ def tile_picked_joinshareduelorder_none_p_kernel(
         half_gm = keep.tile([P, PACK], F32)
         minus_half_gm = keep.tile([P, PACK], F32)
         twice_gn = keep.tile([P, PACK], F32)
-        nc.gpsimd.tensor_scalar(half_gm[:], gm_sb[:], 0.5, 0.0, ALU.mult, ALU.add)
-        nc.gpsimd.tensor_scalar(minus_half_gm[:], gm_sb[:], -0.5, 0.0, ALU.mult, ALU.add)
-        nc.gpsimd.tensor_scalar(twice_gn[:], gn_sb[:], 2.0, 0.0, ALU.mult, ALU.add)
+        nc.scalar.mul(half_gm[:], gm_sb[:], 0.5)
+        nc.scalar.mul(minus_half_gm[:], gm_sb[:], -0.5)
+        nc.scalar.mul(twice_gn[:], gn_sb[:], 2.0)
 
         picked = mx_tiles("picked", S)
         nc.vector.tensor_copy(picked[1][:], table_scales[:].indirect(offs_sb[:]))
+        w1_dealt = keep.tile([P, PACK * H], BF16, align_bytes=64)
+        dst, src = deal_views(w1_dealt, w1_raw)
+        nc.vector.tensor_copy(out=dst[:, :W1_VECTOR_M], in_=src[:, :W1_VECTOR_M])
+        nc.scalar.copy(out=dst[:, W1_VECTOR_M:], in_=src[:, W1_VECTOR_M:])
         w1_mx = mx_tiles("w1", H)
-        for t0, t1, copy in ((0, 2, nc.vector.tensor_copy), (2, PACK, nc.scalar.copy)):
-            w1_dealt = keep.tile([P, (t1 - t0) * PACK * P], BF16, name=f"w1_dealt{t0}", align_bytes=64)
-            copy(
-                out=w1_dealt[:].rearrange("p (t m j) -> p m t j", m=P, j=PACK),
-                in_=w1_raw[:].rearrange("p j (m t) -> p m t j", t=PACK)[:, :, t0:t1],
-            )
-            nc.vector.quantize_mx(
-                out=w1_mx[0][:, P * t0 : P * t1].bitcast(FP8X4), scales=w1_mx[1][:, P * t0 : P * t1], in_=w1_dealt[:]
-            )
+        quantize(w1_mx, w1_dealt, slice(0, H))
         for cols in HALVES:
             nc.vector.tensor_copy(picked[0][:, cols], table_words[:].indirect(entries(offs_sb, cols)))
 
@@ -144,7 +147,7 @@ def tile_picked_joinshareduelorder_none_p_kernel(
             for cols in HALVES if t == 0 else WHOLE:
                 y_acc = psum.tile([P, S], F32, tag="turned", bufs=5)
                 product(y_acc, w1_mx, t, picked, cols, True, True)
-                copy = nc.vector.tensor_copy if t >= 3 else nc.scalar.copy
+                copy = nc.vector.tensor_copy if t >= 4 else nc.scalar.copy
                 copy(out=y[t][:, cols], in_=y_acc[:, cols])
 
         pa, minus_pb, th_turned = (per_tile(name, W) for name in ("pa", "minus_pb", "th_turned"))
@@ -152,6 +155,9 @@ def tile_picked_joinshareduelorder_none_p_kernel(
         for t in tiles:
             nc.vector.tensor_copy(pa[t][:], y[t][:].indirect(n3_sb[:]))
             nc.vector.tensor_scalar(minus_pb[t][:], y[t][:].indirect(n4_sb[:]), -1.0, 0.0, ALU.mult, ALU.add)
+
+        w2_dealt = keep.tile([P, PACK * N], BF16, align_bytes=64)
+        nc.vector.tensor_copy(*deal_views(w2_dealt, w2_raw))
 
         ex, e1, e2 = per_tile("ex", S), per_tile("e1", S), per_tile("e2", S)
 
@@ -223,22 +229,16 @@ def tile_picked_joinshareduelorder_none_p_kernel(
                 nc.vector.tensor_copy(out=z2_planes[:, t, :], in_=z2[t][:])
             else:
                 nc.scalar.copy(out=z2_planes[:, t, :], in_=z2[t][:])
-        dealt = []
-        for t0 in (0, 2):
-            pair = keep.tile([P, 2, 2, PACK * P], BF16, name=f"dealt{t0}", tag=f"root_turned{t0 // 2 + 2}", align_bytes=64)
-            for which, raw in enumerate((w2_raw, w3_raw)):
-                nc.scalar.copy(
-                    out=pair[:, :, which, :].rearrange("p t (m j) -> p m t j", j=PACK),
-                    in_=raw[:].rearrange("p j (m t) -> p m t j", t=PACK)[:, :, t0 : t0 + 2],
-                )
-            dealt.extend(pair[:, i].rearrange("p w c -> p (w c)") for i in range(2))
+        w3_dealt = keep.tile([P, PACK * N], BF16, tag="root_turned3", align_bytes=64)
+        nc.scalar.copy(*deal_views(w3_dealt, w3_raw))
         z2_woven = keep.tile([P, PACK * S], BF16, align_bytes=64)
         z2_mx = mx_tiles("z2", S)
         z_woven = keep.tile([P, PACK * S], BF16, align_bytes=64)
         z_mx = mx_tiles("z", S)
-        first_mx = mx_tiles("w23_first", 2 * P)
+        first_mx = mx_tiles("w2_first", P), mx_tiles("w3_first", P)
         weave(z2_woven, z2_planes, slice(0, S))
-        quantize(first_mx, dealt[0], slice(0, 2 * P))
+        for which, dealt in enumerate((w2_dealt, w3_dealt)):
+            quantize(first_mx[which], dealt, slice(0, P))
         quantize(z2_mx, z2_woven, slice(0, S))
         for cols in PIECES:
             weave(z_woven, z_planes, cols)
@@ -248,21 +248,22 @@ def tile_picked_joinshareduelorder_none_p_kernel(
             keep.tile([P, 6 * P], U32, name="w23_rest_codes", tag="z_planes", align_bytes=64),
             keep.tile([P, 6 * P], U8, name="w23_rest_scales", align_bytes=64),
         )
-        for t in range(1, PACK):
-            cols = slice(2 * P * (t - 1), 2 * P * t)
-            nc.vector.quantize_mx(
-                out=rest_mx[0][:, cols].bitcast(FP8X4),
-                scales=rest_mx[1][:, cols],
-                in_=dealt[t],
-            )
+        for c0, c1 in ((0, P), (P, 3 * P)):
+            for which, dealt in enumerate((w2_dealt, w3_dealt)):
+                cols = slice(3 * P * which + c0, 3 * P * which + c1)
+                nc.vector.quantize_mx(
+                    out=rest_mx[0][:, cols].bitcast(FP8X4),
+                    scales=rest_mx[1][:, cols],
+                    in_=dealt[:, PACK * (P + c0) : PACK * (P + c1)],
+                )
 
         h, result = per_tile("h", S), per_tile("result", S)
         for t in tiles:
-            weights, block = (first_mx, 0) if t == 0 else (rest_mx, 2 * (t - 1))
             for cols in PIECES if t == 0 else WHOLE:
                 h_acc = psum.tile([P, S], F32, tag="turned", bufs=5)
-                product(h_acc, weights, block, z_mx, cols, True, False)
-                product(h_acc, weights, block + 1, z2_mx, cols, False, True)
+                for which, moving in enumerate((z_mx, z2_mx)):
+                    weights, block = (first_mx[which], 0) if t == 0 else (rest_mx, 3 * which + t - 1)
+                    product(h_acc, weights, block, moving, cols, which == 0, which == 1)
                 nc.scalar.copy(out=h[t][:, cols], in_=h_acc[:, cols])
 
         out_rows = out.rearrange("(p t) n -> t p n", t=PACK)

@@ -147,7 +147,7 @@ def tile_picked_joinshareduelorder_none_p_kernel(
             for cols in HALVES if t == 0 else WHOLE:
                 y_acc = psum.tile([P, S], F32, tag="turned", bufs=5)
                 product(y_acc, w1_mx, t, picked, cols, True, True)
-                copy = nc.vector.tensor_copy if t >= 4 else nc.scalar.copy
+                copy = nc.vector.tensor_copy if t >= 3 else nc.scalar.copy
                 copy(out=y[t][:, cols], in_=y_acc[:, cols])
 
         pa, minus_pb, th_turned = (per_tile(name, W) for name in ("pa", "minus_pb", "th_turned"))
@@ -157,7 +157,9 @@ def tile_picked_joinshareduelorder_none_p_kernel(
             nc.vector.tensor_scalar(minus_pb[t][:], y[t][:].indirect(n4_sb[:]), -1.0, 0.0, ALU.mult, ALU.add)
 
         w2_dealt = keep.tile([P, PACK * N], BF16, align_bytes=64)
-        nc.vector.tensor_copy(*deal_views(w2_dealt, w2_raw))
+        dst, src = deal_views(w2_dealt, w2_raw)
+        for m0 in range(0, P, 32):
+            nc.gpsimd.tensor_scalar(dst[:, m0 : m0 + 32], src[:, m0 : m0 + 32], 1.0, 0.0, ALU.mult, ALU.add)
 
         ex, e1, e2 = per_tile("ex", S), per_tile("e1", S), per_tile("e2", S)
 
@@ -261,9 +263,9 @@ def tile_picked_joinshareduelorder_none_p_kernel(
         for t in tiles:
             for cols in PIECES if t == 0 else WHOLE:
                 h_acc = psum.tile([P, S], F32, tag="turned", bufs=5)
-                for which, moving in enumerate((z_mx, z2_mx)):
+                for which, moving in ((1, z2_mx), (0, z_mx)):
                     weights, block = (first_mx[which], 0) if t == 0 else (rest_mx, 3 * which + t - 1)
-                    product(h_acc, weights, block, moving, cols, which == 0, which == 1)
+                    product(h_acc, weights, block, moving, cols, which == 1, which == 0)
                 nc.scalar.copy(out=h[t][:, cols], in_=h_acc[:, cols])
 
         out_rows = out.rearrange("(p t) n -> t p n", t=PACK)

@@ -18,10 +18,16 @@ ACT = mybir.ActivationFunctionType
 
 P = 128
 PACK = 4
-W1_VECTOR_M = 64
+LIST_GROUP = 16
+QUADRANT = 32
+ALIGN = 64
+
 HALVES = (slice(0, S // 2), slice(S // 2, S))
-PIECES = HALVES
 WHOLE = (slice(0, S),)
+W1_VECTOR_PLACES = 64
+FIRST_Y_ON_VECTOR = 2
+GPSIMD_PLACES = 32
+WIDE_BANKS = 5
 
 
 def tile_picked_joinshareduelorder_none_p_kernel(
@@ -34,16 +40,16 @@ def tile_picked_joinshareduelorder_none_p_kernel(
         keep = ctx.enter_context(tc.tile_pool(name="keep", bufs=1))
         psum = ctx.enter_context(tc.psum_pool(name="psum", bufs=PACK))
 
-        def per_tile(name, width, dtype=F32):
-            return [keep.tile([P, width], dtype, name=f"{name}{t}", tag=f"{name}{t}", align_bytes=64) for t in tiles]
+        def row_tiles(name, width):
+            return [keep.tile([P, width], F32, name=f"{name}{t}", tag=f"{name}{t}", align_bytes=ALIGN) for t in tiles]
 
         def load_list(name, src):
             tile = keep.tile(list(src.shape), U16, name=name)
             nc.sync.dma_start(tile[:], src)
             return tile
 
-        def load_weight(name, src, tag):
-            raw = keep.tile([P, PACK, src.shape[1]], F32, name=name, tag=tag, align_bytes=64)
+        def load_weight(name, src):
+            raw = keep.tile([P, PACK, src.shape[1]], F32, name=name, tag=name, align_bytes=ALIGN)
             nc.sync.dma_start(raw[:], src.rearrange("(p j) c -> p j c", j=PACK))
             return raw
 
@@ -52,23 +58,19 @@ def tile_picked_joinshareduelorder_none_p_kernel(
             nc.sync.dma_start(gain[:], src.rearrange("(p t) o -> p (t o)", t=PACK))
             return gain
 
-        def entries(lst, cols):
-            return lst[:, cols.start // 16 : cols.stop // 16]
-
         def mx_tiles(name, width):
-            codes = keep.tile([P, width], U32, name=f"{name}_codes", align_bytes=64)
-            scales = keep.tile([P, width], U8, name=f"{name}_scales", align_bytes=64)
+            codes = keep.tile([P, width], U32, name=f"{name}_codes", align_bytes=ALIGN)
+            scales = keep.tile([P, width], U8, name=f"{name}_scales", align_bytes=ALIGN)
             return codes, scales
 
-        def quantize(mx, src, cols):
+        def quantize(mx, cols, woven, first_col):
+            last_col = first_col + cols.stop - cols.start
             nc.vector.quantize_mx(
-                out=mx[0][:, cols].bitcast(FP8X4),
-                scales=mx[1][:, cols],
-                in_=src[:, PACK * cols.start : PACK * cols.stop],
+                out=mx[0][:, cols].bitcast(FP8X4), scales=mx[1][:, cols], in_=woven[:, PACK * first_col : PACK * last_col]
             )
 
-        def product(acc, weights, t, moving, cols, start, stop):
-            rows = slice(P * t, P * (t + 1))
+        def product(acc, weights, block, moving, cols, start, stop):
+            rows = slice(P * block, P * (block + 1))
             nc.tensor.matmul_mx(
                 out=acc[:, cols],
                 lhsT=weights[0][:, rows].bitcast(FP8X4),
@@ -79,9 +81,9 @@ def tile_picked_joinshareduelorder_none_p_kernel(
                 stop=stop,
             )
 
-        def weave(dst, planes, cols):
-            nc.vector.tensor_copy(
-                out=dst[:, PACK * cols.start : PACK * cols.stop].rearrange("p (c i t) -> p c t i", i=PACK, t=PACK),
+        def weave(copy, woven, planes, cols):
+            copy(
+                out=woven[:, PACK * cols.start : PACK * cols.stop].rearrange("p (c i t) -> p c t i", i=PACK, t=PACK),
                 in_=planes[:, :, cols].rearrange("p t (c i) -> p c t i", i=PACK),
             )
 
@@ -99,28 +101,35 @@ def tile_picked_joinshareduelorder_none_p_kernel(
                 raw[:].rearrange("p j (m t) -> p m t j", t=PACK),
             )
 
-        table_scales = keep.tile([P, T], U8, align_bytes=64)
+        def deal_on_gpsimd(dealt, raw):
+            dst, src = deal_views(dealt, raw)
+            for m0 in range(0, P, GPSIMD_PLACES):
+                ms = slice(m0, m0 + GPSIMD_PLACES)
+                nc.gpsimd.tensor_scalar(dst[:, ms], src[:, ms], 1.0, 0.0, ALU.mult, ALU.add)
+
+        table_scales = keep.tile([P, T], U8, align_bytes=ALIGN)
         nc.vector.memset(table_scales[:].bitcast(I32), 0)
         offs_sb = load_list("offs_sb", offs)
-        w1_raw = load_weight("w1_raw", w1, "w1_raw")
-        for q in range(4):
+        w1_raw = load_weight("w1_raw", w1)
+        for q in range(P // QUADRANT):
             nc.sync.dma_start(
-                table_scales[32 * q : 32 * q + 4, :].bitcast(I32), x_scales[0, 4 * q : 4 * q + 4, :].bitcast(I32)
+                table_scales[QUADRANT * q : QUADRANT * q + 4, :].bitcast(I32),
+                x_scales[0, 4 * q : 4 * q + 4, :].bitcast(I32),
             )
         n3_sb = load_list("n3_sb", n3)
         n4_sb = load_list("n4_sb", n4)
-        table_words = keep.tile([P, T], U32, align_bytes=64)
+        table_words = keep.tile([P, T], U32, align_bytes=ALIGN)
         nc.sync.dma_start(table_words[:].bitcast(I32), x_words[0].rearrange("p n t -> p (n t)").bitcast(I32))
         n1_sb = load_list("n1_sb", n1)
         gm_sb = load_gain("gm_sb", gm)
         n2_sb = load_list("n2_sb", n2)
         gn_sb = load_gain("gn_sb", gn)
-        w2_raw = load_weight("w2_raw", w2, "w2_raw")
-        w3_raw = load_weight("w3_raw", w3, "w3_raw")
+        w2_raw = load_weight("w2_raw", w2)
+        w3_raw = load_weight("w3_raw", w3)
         n5_sb = load_list("n5_sb", n5)
         n6_sb = load_list("n6_sb", n6)
 
-        ident = keep.tile([P, P], F32, align_bytes=64)
+        ident = keep.tile([P, P], F32, align_bytes=ALIGN)
         make_identity(nc, ident[:])
         half_gm = keep.tile([P, PACK], F32)
         minus_half_gm = keep.tile([P, PACK], F32)
@@ -131,78 +140,87 @@ def tile_picked_joinshareduelorder_none_p_kernel(
 
         picked = mx_tiles("picked", S)
         nc.vector.tensor_copy(picked[1][:], table_scales[:].indirect(offs_sb[:]))
-        w1_dealt = keep.tile([P, PACK * H], BF16, align_bytes=64)
+        w1_dealt = keep.tile([P, PACK * H], BF16, align_bytes=ALIGN)
         dst, src = deal_views(w1_dealt, w1_raw)
-        nc.vector.tensor_copy(out=dst[:, :W1_VECTOR_M], in_=src[:, :W1_VECTOR_M])
-        nc.scalar.copy(out=dst[:, W1_VECTOR_M:], in_=src[:, W1_VECTOR_M:])
+        nc.vector.tensor_copy(out=dst[:, :W1_VECTOR_PLACES], in_=src[:, :W1_VECTOR_PLACES])
+        nc.scalar.copy(out=dst[:, W1_VECTOR_PLACES:], in_=src[:, W1_VECTOR_PLACES:])
         w1_mx = mx_tiles("w1", H)
-        quantize(w1_mx, w1_dealt, slice(0, H))
+        quantize(w1_mx, slice(0, H), w1_dealt, 0)
         for cols in HALVES:
-            nc.vector.tensor_copy(picked[0][:, cols], table_words[:].indirect(entries(offs_sb, cols)))
+            entries = offs_sb[:, cols.start // LIST_GROUP : cols.stop // LIST_GROUP]
+            nc.vector.tensor_copy(picked[0][:, cols], table_words[:].indirect(entries))
 
-        y = per_tile("y", 2 * S)
+        y = row_tiles("y", 2 * S)
         for t in tiles:
             nc.gpsimd.memset(y[t][:, S:], 0.0)
+        y_in_psum = {}
         for t in tiles:
             for cols in HALVES if t == 0 else WHOLE:
-                y_acc = psum.tile([P, S], F32, tag="turned", bufs=5)
+                y_acc = psum.tile([P, S], F32, tag="wide", bufs=WIDE_BANKS)
                 product(y_acc, w1_mx, t, picked, cols, True, True)
-                copy = nc.vector.tensor_copy if t >= 3 else nc.scalar.copy
-                copy(out=y[t][:, cols], in_=y_acc[:, cols])
+                if t < FIRST_Y_ON_VECTOR:
+                    nc.scalar.copy(out=y[t][:, cols], in_=y_acc[:, cols])
+                else:
+                    y_in_psum[t] = y_acc
 
-        pa, minus_pb, th_turned = (per_tile(name, W) for name in ("pa", "minus_pb", "th_turned"))
-        share_a, minus_share_b = per_tile("share_a", W), []
+        pa, minus_pb, tanh_turned = (row_tiles(name, W) for name in ("pa", "minus_pb", "tanh_turned"))
+        share_a, minus_share_b = row_tiles("share_a", W), []
         for t in tiles:
             nc.vector.tensor_copy(pa[t][:], y[t][:].indirect(n3_sb[:]))
+            if t + 1 in y_in_psum:
+                nc.vector.tensor_copy(out=y[t + 1][:, :S], in_=y_in_psum[t + 1][:])
             nc.vector.tensor_scalar(minus_pb[t][:], y[t][:].indirect(n4_sb[:]), -1.0, 0.0, ALU.mult, ALU.add)
 
-        w2_dealt = keep.tile([P, PACK * N], BF16, align_bytes=64)
-        dst, src = deal_views(w2_dealt, w2_raw)
-        for m0 in range(0, P, 32):
-            nc.gpsimd.tensor_scalar(dst[:, m0 : m0 + 32], src[:, m0 : m0 + 32], 1.0, 0.0, ALU.mult, ALU.add)
+        w2_dealt = keep.tile([P, PACK * N], BF16, align_bytes=ALIGN)
+        deal_on_gpsimd(w2_dealt, w2_raw)
 
-        ex, e1, e2 = per_tile("ex", S), per_tile("e1", S), per_tile("e2", S)
+        ex, ex_n1, ex_n2 = row_tiles("ex", S), row_tiles("ex_n1", S), row_tiles("ex_n2", S)
 
-        def exp_at(e, lst, t, cols):
-            nc.scalar.activation(e[t][:, cols], y[t][:].indirect(entries(lst, cols)), ACT.Exp, scale=0.5)
+        def exp_at(dst_tiles, offsets, t):
+            nc.scalar.activation(dst_tiles[t][:], y[t][:].indirect(offsets[:]), ACT.Exp, scale=0.5)
 
-        def share_b(t):
-            minus_share_b.append(keep.tile([P, W], F32, name=f"minus_share_b{t}", tag=f"th_turned{t + 1}", align_bytes=64))
+        def make_share_b(t):
+            minus_share_b.append(
+                keep.tile([P, W], F32, name=f"minus_share_b{t}", tag=f"tanh_turned{t + 1}", align_bytes=ALIGN)
+            )
             nc.scalar.activation(
                 minus_share_b[t][:],
-                duel_acc[t][:],
+                tanh_acc[t][:],
                 ACT.Identity,
                 bias=minus_half_gm[:, t : t + 1],
                 scale=half_gm[:, t : t + 1],
             )
 
-        look_ups = [(e, lst, t, WHOLE[0]) for t in tiles for e, lst in ((e1, n1_sb), (e2, n2_sb))]
-        duel_acc = []
+        look_ups = [(dst_tiles, offsets, t) for t in tiles for dst_tiles, offsets in ((ex_n1, n1_sb), (ex_n2, n2_sb))]
+        tanh_acc = []
         for t in tiles:
             col = slice(t, t + 1)
-            lead_acc = psum.tile([P, W], F32, tag="lead", bufs=1)
-            duel_acc.append(psum.tile([P, W], F32, tag="rows", bufs=2, name=f"duel_acc{t}"))
-            turn(lead_acc[:], (pa[t], minus_pb[t]))
-            nc.scalar.activation(th_turned[t][:], lead_acc[:], ACT.Tanh, scale=0.5)
-            turn(duel_acc[t][:], (th_turned[t],))
+            difference_acc = psum.tile([P, W], F32, tag="difference", bufs=1)
+            tanh_acc.append(psum.tile([P, W], F32, tag="tanh", bufs=2, name=f"tanh_acc{t}"))
+            turn(difference_acc[:], (pa[t], minus_pb[t]))
+            nc.scalar.activation(tanh_turned[t][:], difference_acc[:], ACT.Tanh, scale=0.5)
+            turn(tanh_acc[t][:], (tanh_turned[t],))
             exp_at(*look_ups[t])
             nc.scalar.activation(
-                share_a[t][:], duel_acc[t][:], ACT.Identity, bias=half_gm[:, col], scale=half_gm[:, col]
+                share_a[t][:], tanh_acc[t][:], ACT.Identity, bias=half_gm[:, col], scale=half_gm[:, col]
             )
             if t > 0:
-                share_b(t - 1)
+                make_share_b(t - 1)
             nc.scalar.activation(ex[t][:], y[t][:, :S], ACT.Exp, scale=0.5)
-        share_b(PACK - 1)
+        make_share_b(PACK - 1)
+
+        w3_dealt = keep.tile([P, PACK * N], BF16, align_bytes=ALIGN)
+        deal_on_gpsimd(w3_dealt, w3_raw)
 
         sums = []
         for t in tiles:
             for look_up in look_ups[max(2 * t, PACK) : 2 * t + 2]:
                 exp_at(*look_up)
-            sum_acc = psum.tile([P, S], F32, tag="turned", bufs=5)
-            turn(sum_acc[:], (ex[t], e1[t], e2[t]))
+            sum_acc = psum.tile([P, S], F32, tag="wide", bufs=WIDE_BANKS)
+            turn(sum_acc[:], (ex[t], ex_n1[t], ex_n2[t]))
             sums.append(sum_acc)
 
-        z2 = per_tile("z2", S)
+        z2 = row_tiles("z2", S)
         for step in range(PACK + 1):
             if step < PACK:
                 nc.vector.tensor_tensor(z2[step][:].indirect(n3_sb[:]), pa[step][:], share_a[step][:], ALU.mult)
@@ -210,67 +228,56 @@ def tile_picked_joinshareduelorder_none_p_kernel(
                 t = step - 1
                 nc.vector.tensor_tensor(z2[t][:].indirect(n4_sb[:]), minus_pb[t][:], minus_share_b[t][:], ALU.mult)
 
-        root_turned, inverse_turned = per_tile("root_turned", S), per_tile("inverse_turned", S)
-        z_planes = keep.tile([P, PACK, S], BF16, tag="z_planes", align_bytes=64)
+        root_turned, inverse_turned = row_tiles("root_turned", S), row_tiles("inverse_turned", S)
+        z_planes = keep.tile([P, PACK, S], BF16, tag="z_planes", align_bytes=ALIGN)
         for t in tiles:
             nc.scalar.activation(root_turned[t][:], sums[t][:], ACT.Abs_reciprocal_sqrt)
-            back_acc = psum.tile([P, S], F32, tag="turned", bufs=5)
-            gain = twice_gn[:, t : t + 1]
-            if t in ():
-                turn(back_acc[:], (root_turned[t],))
-                nc.vector.scalar_tensor_tensor(inverse_turned[t][:], back_acc[:], gain, ex[t][:], ALU.mult, ALU.mult)
-                nc.vector.tensor_tensor(z_planes[:, t, :], inverse_turned[t][:], back_acc[:], ALU.mult)
-            else:
-                nc.scalar.activation(inverse_turned[t][:], root_turned[t][:], ACT.Square)
-                turn(back_acc[:], (inverse_turned[t],))
-                nc.vector.scalar_tensor_tensor(z_planes[:, t, :], back_acc[:], gain, ex[t][:], ALU.mult, ALU.mult)
+            inverse_acc = psum.tile([P, S], F32, tag="wide", bufs=WIDE_BANKS)
+            nc.scalar.activation(inverse_turned[t][:], root_turned[t][:], ACT.Square)
+            turn(inverse_acc[:], (inverse_turned[t],))
+            nc.vector.scalar_tensor_tensor(
+                z_planes[:, t, :], inverse_acc[:], twice_gn[:, t : t + 1], ex[t][:], ALU.mult, ALU.mult
+            )
 
-        z2_planes = keep.tile([P, PACK, S], BF16, tag="share_a3", align_bytes=64)
+        z2_planes = keep.tile([P, PACK, S], BF16, tag=f"share_a{PACK - 1}", align_bytes=ALIGN)
         for t in tiles:
-            if t < PACK - 0:
-                nc.vector.tensor_copy(out=z2_planes[:, t, :], in_=z2[t][:])
-            else:
-                nc.scalar.copy(out=z2_planes[:, t, :], in_=z2[t][:])
-        w3_dealt = keep.tile([P, PACK * N], BF16, tag="root_turned3", align_bytes=64)
-        nc.scalar.copy(*deal_views(w3_dealt, w3_raw))
-        z2_woven = keep.tile([P, PACK * S], BF16, align_bytes=64)
+            nc.vector.tensor_copy(out=z2_planes[:, t, :], in_=z2[t][:])
+        z2_woven = keep.tile([P, PACK * S], BF16, tag=f"root_turned{PACK - 1}", align_bytes=ALIGN)
         z2_mx = mx_tiles("z2", S)
-        z_woven = keep.tile([P, PACK * S], BF16, align_bytes=64)
+        z_woven = keep.tile([P, PACK * S], BF16, align_bytes=ALIGN)
         z_mx = mx_tiles("z", S)
+        dealt = (w2_dealt, w3_dealt)
         first_mx = mx_tiles("w2_first", P), mx_tiles("w3_first", P)
-        weave(z2_woven, z2_planes, slice(0, S))
-        for which, dealt in enumerate((w2_dealt, w3_dealt)):
-            quantize(first_mx[which], dealt, slice(0, P))
-        quantize(z2_mx, z2_woven, slice(0, S))
-        for cols in PIECES:
-            weave(z_woven, z_planes, cols)
-        for cols in PIECES:
-            quantize(z_mx, z_woven, cols)
-        rest_mx = (
-            keep.tile([P, 6 * P], U32, name="w23_rest_codes", tag="z_planes", align_bytes=64),
-            keep.tile([P, 6 * P], U8, name="w23_rest_scales", align_bytes=64),
-        )
-        for c0, c1 in ((0, P), (P, 3 * P)):
-            for which, dealt in enumerate((w2_dealt, w3_dealt)):
-                cols = slice(3 * P * which + c0, 3 * P * which + c1)
-                nc.vector.quantize_mx(
-                    out=rest_mx[0][:, cols].bitcast(FP8X4),
-                    scales=rest_mx[1][:, cols],
-                    in_=dealt[:, PACK * (P + c0) : PACK * (P + c1)],
-                )
+        for cols in HALVES:
+            weave(nc.scalar.copy, z2_woven, z2_planes, cols)
+        for which in range(2):
+            quantize(first_mx[which], slice(0, P), dealt[which], 0)
+        for cols in HALVES:
+            weave(nc.vector.tensor_copy, z_woven, z_planes, cols)
+        for cols in HALVES:
+            quantize(z2_mx, cols, z2_woven, cols.start)
+            quantize(z_mx, cols, z_woven, cols.start)
 
-        h, result = per_tile("h", S), per_tile("result", S)
+        rest = N - P
+        rest_mx = (
+            keep.tile([P, 2 * rest], U32, name="rest_codes", tag="z_planes", align_bytes=ALIGN),
+            keep.tile([P, 2 * rest], U8, name="rest_scales", align_bytes=ALIGN),
+        )
+        for c0, c1 in ((0, P), (P, rest)):
+            for which in range(2):
+                quantize(rest_mx, slice(rest * which + c0, rest * which + c1), dealt[which], P + c0)
+
+        h, result = row_tiles("h", S), row_tiles("result", S)
         for t in tiles:
-            for cols in PIECES if t == 0 else WHOLE:
-                h_acc = psum.tile([P, S], F32, tag="turned", bufs=5)
+            for cols in HALVES if t == 0 else WHOLE:
+                h_acc = psum.tile([P, S], F32, tag="wide", bufs=WIDE_BANKS)
                 for which, moving in ((1, z2_mx), (0, z_mx)):
-                    weights, block = (first_mx[which], 0) if t == 0 else (rest_mx, 3 * which + t - 1)
+                    weights, block = (first_mx[which], 0) if t == 0 else (rest_mx, (PACK - 1) * which + t - 1)
                     product(h_acc, weights, block, moving, cols, which == 1, which == 0)
                 nc.scalar.copy(out=h[t][:, cols], in_=h_acc[:, cols])
 
         out_rows = out.rearrange("(p t) n -> t p n", t=PACK)
-
-        pa2, lead, rise, drop, fall = (per_tile(name, W) for name in ("pa2", "lead", "rise", "drop", "fall"))
+        pa2, lead, rise, drop, fall = (row_tiles(name, W) for name in ("pa2", "lead", "rise", "drop", "fall"))
         for t in tiles:
             nc.vector.tensor_copy(pa2[t][:], h[t][:].indirect(n5_sb[:]))
             nc.vector.tensor_tensor(lead[t][:], h[t][:].indirect(n6_sb[:]), pa2[t][:], ALU.subtract)

from contextlib import ExitStack

import concourse.mybir as mybir
from concourse.masks import make_identity

K, T, S, H, N, W = 512, 2048, 512, 512, 512, 256
FLOPS = 2 * K * H * S + 2 * 2 * H * N * S

F32 = mybir.dt.float32
BF16 = mybir.dt.bfloat16
I32 = mybir.dt.int32
U32 = mybir.dt.uint32
U16 = mybir.dt.uint16
U8 = mybir.dt.uint8
FP8X4 = mybir.dt.float8_e4m3fn_x4
ALU = mybir.AluOpType
ACT = mybir.ActivationFunctionType

P = 128
PACK = 4
LIST_GROUP = 16
QUADRANT = 32
ALIGN = 64

HALVES = (slice(0, S // 2), slice(S // 2, S))
WHOLE = (slice(0, S),)
W1_VECTOR_PLACES = 64
FIRST_Y_ON_VECTOR = 2
GPSIMD_PLACES = 32
WIDE_BANKS = 5


def tile_picked_joinshareduelorder_none_p_kernel(
    tc, x_words, x_scales, w1, gn, gm, w2, w3, offs, n1, n2, n3, n4, n5, n6, out
):
    nc = tc.nc
    tiles = range(PACK)

    with ExitStack() as ctx:
        keep = ctx.enter_context(tc.tile_pool(name="keep", bufs=1))
        psum = ctx.enter_context(tc.psum_pool(name="psum", bufs=PACK))

        def row_tiles(name, width):
            return [keep.tile([P, width], F32, name=f"{name}{t}", tag=f"{name}{t}", align_bytes=ALIGN) for t in tiles]

        def load_list(name, src):
            tile = keep.tile(list(src.shape), U16, name=name)
            nc.sync.dma_start(tile[:], src)
            return tile

        def load_weight(name, src):
            raw = keep.tile([P, PACK, src.shape[1]], F32, name=name, tag=name, align_bytes=ALIGN)
            nc.sync.dma_start(raw[:], src.rearrange("(p j) c -> p j c", j=PACK))
            return raw

        def load_gain(name, src):
            gain = keep.tile([P, PACK], F32, name=name)
            nc.sync.dma_start(gain[:], src.rearrange("(p t) o -> p (t o)", t=PACK))
            return gain

        def mx_tiles(name, width):
            codes = keep.tile([P, width], U32, name=f"{name}_codes", align_bytes=ALIGN)
            scales = keep.tile([P, width], U8, name=f"{name}_scales", align_bytes=ALIGN)
            return codes, scales

        def quantize(mx, cols, woven, first_col):
            last_col = first_col + cols.stop - cols.start
            nc.vector.quantize_mx(
                out=mx[0][:, cols].bitcast(FP8X4), scales=mx[1][:, cols], in_=woven[:, PACK * first_col : PACK * last_col]
            )

        def product(acc, weights, block, moving, cols, start, stop):
            rows = slice(P * block, P * (block + 1))
            nc.tensor.matmul_mx(
                out=acc[:, cols],
                lhsT=weights[0][:, rows].bitcast(FP8X4),
                lhsT_scale=weights[1][:, rows],
                rhs=moving[0][:, cols].bitcast(FP8X4),
                rhs_scale=moving[1][:, cols],
                start=start,
                stop=stop,
            )

        def weave(copy, woven, planes, cols):
            copy(
                out=woven[:, PACK * cols.start : PACK * cols.stop].rearrange("p (c i t) -> p c t i", i=PACK, t=PACK),
                in_=planes[:, :, cols].rearrange("p t (c i) -> p c t i", i=PACK),
            )

        def turn(acc, terms):
            for b in range(acc.shape[1] // P):
                cols = slice(P * b, P * (b + 1))
                for i, term in enumerate(terms):
                    nc.tensor.matmul(
                        acc[:, cols], term[:, cols], ident[:], start=i == 0, stop=i == len(terms) - 1, is_transpose=True
                    )

        def deal_views(dealt, raw):
            return (
                dealt[:].rearrange("p (t m j) -> p m t j", t=PACK, j=PACK),
                raw[:].rearrange("p j (m t) -> p m t j", t=PACK),
            )

        def deal_on_gpsimd(dealt, raw):
            dst, src = deal_views(dealt, raw)
            for m0 in range(0, P, GPSIMD_PLACES):
                ms = slice(m0, m0 + GPSIMD_PLACES)
                nc.gpsimd.tensor_scalar(dst[:, ms], src[:, ms], 1.0, 0.0, ALU.mult, ALU.add)

        table_scales = keep.tile([P, T], U8, align_bytes=ALIGN)
        nc.vector.memset(table_scales[:].bitcast(I32), 0)
        offs_sb = load_list("offs_sb", offs)
        w1_raw = load_weight("w1_raw", w1)
        for q in range(P // QUADRANT):
            nc.sync.dma_start(
                table_scales[QUADRANT * q : QUADRANT * q + 4, :].bitcast(I32),
                x_scales[0, 4 * q : 4 * q + 4, :].bitcast(I32),
            )
        n3_sb = load_list("n3_sb", n3)
        n4_sb = load_list("n4_sb", n4)
        table_words = keep.tile([P, T], U32, align_bytes=ALIGN)
        nc.sync.dma_start(table_words[:].bitcast(I32), x_words[0].rearrange("p n t -> p (n t)").bitcast(I32))
        n1_sb = load_list("n1_sb", n1)
        gm_sb = load_gain("gm_sb", gm)
        n2_sb = load_list("n2_sb", n2)
        gn_sb = load_gain("gn_sb", gn)
        w2_raw = load_weight("w2_raw", w2)
        w3_raw = load_weight("w3_raw", w3)
        n5_sb = load_list("n5_sb", n5)
        n6_sb = load_list("n6_sb", n6)

        ident = keep.tile([P, P], F32, align_bytes=ALIGN)
        make_identity(nc, ident[:])
        half_gm = keep.tile([P, PACK], F32)
        minus_half_gm = keep.tile([P, PACK], F32)
        twice_gn = keep.tile([P, PACK], F32)
        nc.scalar.mul(half_gm[:], gm_sb[:], 0.5)
        nc.scalar.mul(minus_half_gm[:], gm_sb[:], -0.5)
        nc.scalar.mul(twice_gn[:], gn_sb[:], 2.0)

        picked = mx_tiles("picked", S)
        nc.vector.tensor_copy(picked[1][:], table_scales[:].indirect(offs_sb[:]))
        w1_dealt = keep.tile([P, PACK * H], BF16, align_bytes=ALIGN)
        dst, src = deal_views(w1_dealt, w1_raw)
        nc.vector.tensor_copy(out=dst[:, :W1_VECTOR_PLACES], in_=src[:, :W1_VECTOR_PLACES])
        nc.scalar.copy(out=dst[:, W1_VECTOR_PLACES:], in_=src[:, W1_VECTOR_PLACES:])
        w1_mx = mx_tiles("w1", H)
        quantize(w1_mx, slice(0, H), w1_dealt, 0)
        for cols in HALVES:
            entries = offs_sb[:, cols.start // LIST_GROUP : cols.stop // LIST_GROUP]
            nc.vector.tensor_copy(picked[0][:, cols], table_words[:].indirect(entries))

        y = row_tiles("y", 2 * S)
        for t in tiles:
            nc.gpsimd.memset(y[t][:, S:], 0.0)
        y_in_psum = {}
        for t in tiles:
            for cols in HALVES if t == 0 else WHOLE:
                y_acc = psum.tile([P, S], F32, tag="wide", bufs=WIDE_BANKS)
                product(y_acc, w1_mx, t, picked, cols, True, True)
                if t < FIRST_Y_ON_VECTOR:
                    nc.scalar.copy(out=y[t][:, cols], in_=y_acc[:, cols])
                else:
                    y_in_psum[t] = y_acc

        pa, minus_pb, tanh_turned = (row_tiles(name, W) for name in ("pa", "minus_pb", "tanh_turned"))
        share_a, minus_share_b = row_tiles("share_a", W), []
        for t in tiles:
            nc.vector.tensor_copy(pa[t][:], y[t][:].indirect(n3_sb[:]))
            if t + 1 in y_in_psum:
                nc.vector.tensor_copy(out=y[t + 1][:, :S], in_=y_in_psum[t + 1][:])
            nc.vector.tensor_scalar(minus_pb[t][:], y[t][:].indirect(n4_sb[:]), -1.0, 0.0, ALU.mult, ALU.add)

        w2_dealt = keep.tile([P, PACK * N], BF16, align_bytes=ALIGN)
        deal_on_gpsimd(w2_dealt, w2_raw)

        ex, ex_n1, ex_n2 = row_tiles("ex", S), row_tiles("ex_n1", S), row_tiles("ex_n2", S)

        def exp_at(dst_tiles, offsets, t):
            nc.scalar.activation(dst_tiles[t][:], y[t][:].indirect(offsets[:]), ACT.Exp, scale=0.5)

        def make_share_b(t):
            minus_share_b.append(
                keep.tile([P, W], F32, name=f"minus_share_b{t}", tag=f"tanh_turned{t + 1}", align_bytes=ALIGN)
            )
            nc.scalar.activation(
                minus_share_b[t][:],
                tanh_acc[t][:],
                ACT.Identity,
                bias=minus_half_gm[:, t : t + 1],
                scale=half_gm[:, t : t + 1],
            )

        look_ups = [(dst_tiles, offsets, t) for t in tiles for dst_tiles, offsets in ((ex_n1, n1_sb), (ex_n2, n2_sb))]
        tanh_acc = []
        for t in tiles:
            col = slice(t, t + 1)
            difference_acc = psum.tile([P, W], F32, tag="difference", bufs=1)
            tanh_acc.append(psum.tile([P, W], F32, tag="tanh", bufs=2, name=f"tanh_acc{t}"))
            turn(difference_acc[:], (pa[t], minus_pb[t]))
            nc.scalar.activation(tanh_turned[t][:], difference_acc[:], ACT.Tanh, scale=0.5)
            turn(tanh_acc[t][:], (tanh_turned[t],))
            exp_at(*look_ups[t])
            nc.scalar.activation(
                share_a[t][:], tanh_acc[t][:], ACT.Identity, bias=half_gm[:, col], scale=half_gm[:, col]
            )
            if t > 0:
                make_share_b(t - 1)
            nc.scalar.activation(ex[t][:], y[t][:, :S], ACT.Exp, scale=0.5)
        make_share_b(PACK - 1)

        w3_dealt = keep.tile([P, PACK * N], BF16, align_bytes=ALIGN)
        deal_on_gpsimd(w3_dealt, w3_raw)

        sums = []
        for t in tiles:
            for look_up in look_ups[max(2 * t, PACK) : 2 * t + 2]:
                exp_at(*look_up)
            sum_acc = psum.tile([P, S], F32, tag="wide", bufs=WIDE_BANKS)
            turn(sum_acc[:], (ex[t], ex_n1[t], ex_n2[t]))
            sums.append(sum_acc)

        z2 = row_tiles("z2", S)
        for step in range(PACK + 1):
            if step < PACK:
                nc.vector.tensor_tensor(z2[step][:].indirect(n3_sb[:]), pa[step][:], share_a[step][:], ALU.mult)
            if step > 0:
                t = step - 1
                nc.vector.tensor_tensor(z2[t][:].indirect(n4_sb[:]), minus_pb[t][:], minus_share_b[t][:], ALU.mult)

        root_turned, inverse_turned = row_tiles("root_turned", S), row_tiles("inverse_turned", S)
        z_planes = keep.tile([P, PACK, S], BF16, tag="z_planes", align_bytes=ALIGN)
        for t in tiles:
            nc.scalar.activation(root_turned[t][:], sums[t][:], ACT.Abs_reciprocal_sqrt)
            inverse_acc = psum.tile([P, S], F32, tag="wide", bufs=WIDE_BANKS)
            nc.scalar.activation(inverse_turned[t][:], root_turned[t][:], ACT.Square)
            turn(inverse_acc[:], (inverse_turned[t],))
            nc.vector.scalar_tensor_tensor(
                z_planes[:, t, :], inverse_acc[:], twice_gn[:, t : t + 1], ex[t][:], ALU.mult, ALU.mult
            )

        z2_planes = keep.tile([P, PACK, S], BF16, tag=f"share_a{PACK - 1}", align_bytes=ALIGN)
        for t in tiles:
            nc.vector.tensor_copy(out=z2_planes[:, t, :], in_=z2[t][:])
        z2_woven = keep.tile([P, PACK * S], BF16, tag=f"root_turned{PACK - 1}", align_bytes=ALIGN)
        z2_mx = mx_tiles("z2", S)
        z_woven = keep.tile([P, PACK * S], BF16, align_bytes=ALIGN)
        z_mx = mx_tiles("z", S)
        dealt = (w2_dealt, w3_dealt)
        first_mx = mx_tiles("w2_first", P), mx_tiles("w3_first", P)
        for cols in HALVES:
            weave(nc.scalar.copy, z2_woven, z2_planes, cols)
        for which in range(2):
            quantize(first_mx[which], slice(0, P), dealt[which], 0)
        for cols in HALVES:
            weave(nc.vector.tensor_copy, z_woven, z_planes, cols)
        for cols in HALVES:
            quantize(z2_mx, cols, z2_woven, cols.start)
            quantize(z_mx, cols, z_woven, cols.start)

        rest = N - P
        rest_mx = (
            keep.tile([P, 2 * rest], U32, name="rest_codes", tag="z_planes", align_bytes=ALIGN),
            keep.tile([P, 2 * rest], U8, name="rest_scales", align_bytes=ALIGN),
        )
        for c0, c1 in ((0, P), (P, rest)):
            for which in range(2):
                quantize(rest_mx, slice(rest * which + c0, rest * which + c1), dealt[which], P + c0)

        h, result = row_tiles("h", S), row_tiles("result", S)
        for t in tiles:
            for cols in HALVES if t == 0 else WHOLE:
                h_acc = psum.tile([P, S], F32, tag="wide", bufs=WIDE_BANKS)
                for which, moving in ((1, z2_mx), (0, z_mx)):
                    weights, block = (first_mx[which], 0) if t == 0 else (rest_mx, (PACK - 1) * which + t - 1)
                    product(h_acc, weights, block, moving, cols, which == 1, which == 0)
                nc.scalar.copy(out=h[t][:, cols], in_=h_acc[:, cols])

        out_rows = out.rearrange("(p t) n -> t p n", t=PACK)
        pa2, lead, rise, drop, fall = (row_tiles(name, W) for name in ("pa2", "lead", "rise", "drop", "fall"))
        for t in tiles:
            nc.vector.tensor_copy(pa2[t][:], h[t][:].indirect(n5_sb[:]))
            nc.vector.tensor_tensor(lead[t][:], h[t][:].indirect(n6_sb[:]), pa2[t][:], ALU.subtract)
            nc.scalar.activation(rise[t][:], lead[t][:], ACT.Relu)
            nc.scalar.activation(drop[t][:], lead[t][:], ACT.Relu, scale=-1.0)
            nc.scalar.mul(fall[t][:], drop[t][:], -1.0)
        for step in range(PACK + 1):
            if step < PACK:
                nc.vector.tensor_tensor(result[step][:].indirect(n5_sb[:]), pa2[step][:], rise[step][:], ALU.add)
            if step > 0:
                t = step - 1
                nc.vector.tensor_tensor(result[t][:].indirect(n6_sb[:]), pa2[t][:], fall[t][:], ALU.add)
                nc.sync.dma_start(out_rows[t], result[t][:])
